import numpy as np
import ml_dtypes


def mxq(x, axis, fmt="e4m3"):
    dtype, down = {"e4m3": (ml_dtypes.float8_e4m3fn, 7), "e5m2": (ml_dtypes.float8_e5m2, 14)}[fmt]
    v = np.moveaxis(np.asarray(x, np.float32).astype(ml_dtypes.bfloat16).astype(np.float64), axis, -1)
    blocks = v.reshape(v.shape[:-1] + (-1, 32))
    amax = np.abs(blocks).max(-1, keepdims=True)
    byte = np.maximum(np.where(amax > 0, np.frexp(amax)[1] - 1 + 127, 0) - down, 1)
    scale = np.exp2(byte - 127.0)
    codes = (blocks / scale).astype(np.float32).astype(dtype).astype(np.float64)
    return np.moveaxis((codes * scale).reshape(v.shape), -1, axis)


WIDE = False


def mx_kscale(k):
    if not WIDE:
        return np.ones(k)
    levels = np.array([10, -10, 5, -5, 0])
    if k % 512:
        return np.exp2(np.random.permutation(np.resize(levels, k // 32))).repeat(32)
    a = np.empty((k // 512, 16))
    for p in range(k // 512):
        a[p, :8] = np.random.permutation(np.resize(levels, 8))
        for g in range(8):
            far = levels[np.abs(levels - a[p, g]) >= 10]
            a[p, g + 8] = far[np.random.randint(len(far))]
    return np.exp2(a.ravel()).repeat(32)


def f64(x):
    return np.asarray(x).astype(np.float64)


def striped(idx):
    return np.tile(np.asarray(idx).reshape(-1, 16).T, (8, 1)).astype(np.uint16)


def unstriped(offs):
    return offs[:16].T.reshape(-1).astype(np.int64)


E2M1 = np.array([0.0, 0.5, 1.0, 1.5, 2.0, 3.0, 4.0, 6.0, -0.0, -0.5, -1.0, -1.5, -2.0, -3.0, -4.0, -6.0])


def pack_weight(w, fmt):
    k, n = w.shape
    w = f64(np.asarray(w, np.float32).astype(ml_dtypes.bfloat16)).reshape(k // 32, 32, n)
    amax = np.abs(w).max(1)
    if fmt == "e4m3":
        byte = np.frexp(amax)[1] - 1 + 127 - 7
    else:
        mant, ex = np.frexp(amax / 6.0)
        byte = np.where(mant > 0.5, ex, ex - 1) + 127
    byte = np.clip(np.where(amax > 0, byte, 1), 1, 254)
    scaled = (w * np.exp2(127.0 - byte)[:, None, :]).reshape(k, n).astype(np.float32)
    by_word = np.ascontiguousarray(scaled.reshape(k // 512, 128, 4, n).transpose(0, 1, 3, 2))
    if fmt == "e4m3":
        words = by_word.astype(ml_dtypes.float8_e4m3fn).view(np.uint8)
    else:
        c = by_word.astype(ml_dtypes.float4_e2m1fn).view(np.uint8) & 0xF
        words = (c[..., 0::2] | (c[..., 1::2] << 4)).reshape(k // 512, 128, 2 * n)
    return np.ascontiguousarray(words), np.ascontiguousarray(byte.astype(np.uint8).reshape(k // 512, 16, n))


def unpack_weight(words, scales, fmt):
    g, _, n = scales.shape
    words = np.ascontiguousarray(words).reshape(g, 128, n, -1)
    if fmt == "e4m3":
        vals = words.view(ml_dtypes.float8_e4m3fn).astype(np.float64)
    else:
        nib = np.empty((g, 128, n, 4), np.uint8)
        nib[..., 0::2] = words & 0xF
        nib[..., 1::2] = words >> 4
        vals = E2M1[nib]
    vals = vals * np.repeat(np.exp2(scales.astype(np.float64) - 127.0), 8, axis=1)[..., None]
    return vals.transpose(0, 1, 3, 2).reshape(g * 512, n)


def bf(x):
    return np.asarray(x, np.float32).astype(ml_dtypes.bfloat16)


def planes(Y):
    r, m = Y.shape
    b = f64(bf(Y)).reshape(r // 32, 32, m)
    amax = np.abs(b).max(1)
    byte = np.clip(np.where(amax > 0, np.frexp(amax)[1] - 1 + 127 - 7, 1), 1, 254)
    codes = (b * np.exp2(127.0 - byte)[:, None, :]).reshape(r, m).astype(np.float32).astype(ml_dtypes.float8_e4m3fn).view(np.uint8)
    words = codes.reshape(r // 512, 128, 4, m).transpose(0, 1, 3, 2)
    return np.ascontiguousarray(words), np.ascontiguousarray(byte.astype(np.uint8).reshape(r // 512, 16, m))


K, T, J, N = 512, 2048, 512, 512


def setup_inputs():
    n = np.random.standard_normal
    idx = np.random.permutation(T)[:J]
    fk = mx_kscale(K)
    wp = pack_weight(n((K, N)) * 1 / np.sqrt(K) * fk[:, None], "e4m3")
    return {
        "xf": (n((K, T)) / fk[:, None]).astype(np.float32),
        "ta": (np.random.uniform(0.5, 2.0, (K, 1))).astype(np.float32),
        "tb": (np.random.uniform(-1.0, 1.0, (K, 1))).astype(np.float32),
        "td": (np.random.uniform(-0.7, 0.7, (K, 1))).astype(np.float32),
        "w_words": wp[0],
        "w_scales": wp[1],
        "rw": (np.random.uniform(0.5, 2.0, (1, J))).astype(np.float32),
        "offs": striped(idx),
    }


def reference(xf, ta, tb, td, w_words, w_scales, rw, offs):
    idx = unstriped(offs)
    wu = unpack_weight(w_words, w_scales, "e4m3")
    xg = f64(xf)[:, idx]
    x1 = np.pad(xg, ((0, 0), (1, 0)))[:, :J]
    x2 = np.pad(xg, ((0, 0), (2, 0)))[:, :J]
    u = f64(ta) * xg + f64(tb) * x1 + f64(td) * x2
    uq = mxq(u, 0, "e4m3")
    p = wu.T @ uq
    y = np.maximum(p, 0.0) * f64(rw)
    words, scales = planes(y)
    return y, words, scales

@@ -1,0 +1,169 @@
+from contextlib import ExitStack
+
+import concourse.mybir as mybir
+from concourse.masks import make_identity
+
+K, T, J, N = 512, 2048, 512, 512
+FLOPS = 2 * K * J * N
+
+F32 = mybir.dt.float32
+BF16 = mybir.dt.bfloat16
+I32 = mybir.dt.int32
+U32 = mybir.dt.uint32
+U16 = mybir.dt.uint16
+U8 = mybir.dt.uint8
+FP8X4 = mybir.dt.float8_e4m3fn_x4
+MULT = mybir.AluOpType.mult
+ADD = mybir.AluOpType.add
+MAX = mybir.AluOpType.max
+COPY = mybir.ActivationFunctionType.Copy
+
+P = 128
+PACK = 4
+PAD = 4
+HALF = J // 2
+CHUNK = 128
+LIST_ROWS = 16
+
+
+def tile_moe_expert_with_taps_pl_kernel(tc, xf, ta, tb, td, w_words, w_scales, rw, offs, out_0, out_1, out_2):
+    nc = tc.nc
+    with ExitStack() as ctx:
+        keep = ctx.enter_context(tc.tile_pool(name="keep", bufs=1))
+        psum = ctx.enter_context(tc.psum_pool(name="psum", bufs=1))
+
+        offsets = keep.tile([P, J // LIST_ROWS], U16, name="offsets")
+        x_rows = xf.rearrange("(p t) c -> p t c", t=PACK)
+        window = [keep.tile([P, T], F32, name=f"window{t}") for t in range(PACK)]
+        w_raw = keep.tile([P, N], I32, name="w_raw")
+        ta_sb = keep.tile([P, PACK], F32, name="ta_sb")
+        tb_sb = keep.tile([P, PACK], F32, name="tb_sb")
+        td_sb = keep.tile([P, PACK], F32, name="td_sb")
+        rw_col = keep.tile([P, PACK], F32, name="rw_col")
+        ws_raw = keep.tile([P, N], U8, name="ws_raw")
+        zeros = keep.tile([P, PAD], F32, name="zeros")
+        nc.vector.memset(zeros[:], 0.0)
+        nc.vector.memset(ws_raw[:].bitcast(I32), 0)
+        nc.sync.dma_start(offsets[:], offs)
+        for t in range(PACK):
+            nc.sync.dma_start(window[t][:], x_rows[:, t, :])
+        nc.sync.dma_start(w_raw[:], w_words[0].rearrange("p n t -> p (n t)").bitcast(I32))
+        nc.scalar.dma_start(ta_sb[:], ta.rearrange("(p t) o -> p (t o)", t=PACK))
+        nc.scalar.dma_start(tb_sb[:], tb.rearrange("(p t) o -> p (t o)", t=PACK))
+        nc.gpsimd.dma_start(td_sb[:], td.rearrange("(p t) o -> p (t o)", t=PACK))
+        nc.gpsimd.dma_start(rw_col[:], rw.rearrange("o (n m) -> (o n) m", m=PACK))
+        xg = [keep.tile([P, PAD + J], F32, name=f"xg{t}") for t in range(PACK)]
+        for t in range(PACK):
+            nc.scalar.activation(xg[t][:, 0:PAD], zeros[:], COPY)
+        for q in range(4):
+            nc.scalar.dma_start(ws_raw[32 * q : 32 * q + 4, :].bitcast(I32), w_scales[0, 4 * q : 4 * q + 4, :].bitcast(I32))
+        ident = keep.tile([P, P], F32, name="ident")
+        make_identity(nc, ident[:])
+
+        rw_ps = psum.tile([P, PACK, P], F32, name="rw_ps")
+        for m in range(PACK):
+            nc.tensor.transpose(rw_ps[:, m, :], rw_col[:, m : m + 1].to_broadcast([P, P]), ident[:])
+        rw_all = keep.tile([P, J], F32, name="rw_all")
+        nc.scalar.copy(rw_all[:].rearrange("p (n m) -> p n m", m=PACK), rw_ps[:].rearrange("p m n -> p n m"))
+
+        w_scale = keep.tile([P, N], U8, name="w_scale", align_bytes=64)
+        nc.vector.tensor_copy(
+            w_scale[:].rearrange("p (t m) -> p m t", t=PACK), ws_raw[:].rearrange("p (m t) -> p m t", t=PACK)
+        )
+
+        own = [keep.tile([P, J], F32, name=f"own{t}") for t in range(PACK)]
+        near = [keep.tile([P, PACK, HALF], F32, name=f"near{h}") for h in range(2)]
+        far = [keep.tile([P, PACK, HALF], F32, name=f"far{h}") for h in range(2)]
+        w_code = keep.tile([P, N], I32, name="w_code", align_bytes=64)
+
+        for t in range(PACK):
+            for h in range(2):
+                j0, j1 = h * HALF, (h + 1) * HALF
+                nc.vector.tensor_copy(
+                    xg[t][:, PAD + j0 : PAD + j1], window[t][:].indirect(offsets[:, j0 // LIST_ROWS : j1 // LIST_ROWS])
+                )
+            for h in range(2):
+                j0, j1 = h * HALF, (h + 1) * HALF
+                nc.scalar.activation(own[t][:, j0:j1], xg[t][:, PAD + j0 : PAD + j1], COPY, scale=ta_sb[:, t : t + 1])
+                nc.vector.scalar_tensor_tensor(
+                    near[h][:, t, :], xg[t][:, PAD - 1 + j0 : PAD - 1 + j1], tb_sb[:, t : t + 1], own[t][:, j0:j1], MULT, ADD
+                )
+            for h in range(2):
+                j0, j1 = h * HALF, (h + 1) * HALF
+                nc.scalar.activation(far[h][:, t, :], xg[t][:, PAD - 2 + j0 : PAD - 2 + j1], COPY, scale=td_sb[:, t : t + 1])
+
+        nc.vector.tensor_copy(
+            w_code[:].rearrange("p (t m) -> p m t", t=PACK), w_raw[:].rearrange("p (m t) -> p m t", t=PACK)
+        )
+
+        chunks = J // CHUNK
+        u_code = [keep.tile([P, CHUNK], U32, name=f"u_code{c}", align_bytes=64) for c in range(chunks)]
+        u_scale = [keep.tile([P, CHUNK], U8, name=f"u_scale{c}", align_bytes=64) for c in range(chunks)]
+
+        def quantize_u(c):
+            h, c0 = divmod(c * CHUNK, HALF)
+            u_words = keep.tile([P, CHUNK, PACK], BF16, name=f"u_words{c}", align_bytes=64)
+            nc.vector.tensor_tensor(
+                u_words[:].rearrange("p (c i) t -> p c t i", i=4),
+                near[h][:, :, c0 : c0 + CHUNK].rearrange("p t (c i) -> p c t i", i=4),
+                far[h][:, :, c0 : c0 + CHUNK].rearrange("p t (c i) -> p c t i", i=4),
+                ADD,
+            )
+            nc.vector.quantize_mx(
+                out=u_code[c][:].bitcast(FP8X4), scales=u_scale[c][:], in_=u_words[:].rearrange("p j t -> p (j t)")
+            )
+
+        y_rows = out_0.rearrange("(p t) j -> p t j", t=PACK)
+        y_code = keep.tile([P, J], U32, name="y_code", align_bytes=64)
+        y_scale = keep.tile([P, J], U8, name="y_scale", align_bytes=64)
+        code_rows = out_1[0].rearrange("p j t -> p (j t)").bitcast(I32)
+        y_words = []
+
+        def product(c):
+            acc = psum.tile([P, PACK, CHUNK], F32, name=f"acc{c}")
+            for t in range(PACK):
+                nc.tensor.matmul_mx(
+                    out=acc[:, t, :],
+                    lhsT=w_code[:, t * P : (t + 1) * P].bitcast(FP8X4),
+                    lhsT_scale=w_scale[:, t * P : (t + 1) * P],
+                    rhs=u_code[c][:].bitcast(FP8X4),
+                    rhs_scale=u_scale[c][:],
+                    start=True,
+                    stop=True,
+                )
+            cols = slice(c * CHUNK, (c + 1) * CHUNK)
+            y = keep.tile([P, PACK, CHUNK], F32, name=f"y{c}")
+            nc.vector.scalar_tensor_tensor(
+                y[:], acc[:], 0.0, rw_all[:, cols].unsqueeze(1).to_broadcast([P, PACK, CHUNK]), MAX, MULT
+            )
+            nc.sync.dma_start(y_rows[:, :, cols], y[:])
+            words = keep.tile([P, CHUNK, PACK], BF16, name=f"y_words{c}", align_bytes=64)
+            dst = words[:].rearrange("p (c i) t -> p c t i", i=4)
+            src = y[:].rearrange("p t (c i) -> p c t i", i=4)
+            if c < chunks - 1:
+                nc.scalar.copy(dst, src)
+            else:
+                nc.vector.tensor_copy(dst, src)
+            y_words.append(words)
+
+        def quantize_y(c):
+            cols = slice(c * CHUNK, (c + 1) * CHUNK)
+            nc.vector.quantize_mx(
+                out=y_code[:, cols].bitcast(FP8X4), scales=y_scale[:, cols], in_=y_words[c][:].rearrange("p j t -> p (j t)")
+            )
+
+        for c in range(chunks):
+            quantize_u(c)
+        product(0)
+        product(1)
+        product(2)
+        quantize_y(0)
+        quantize_y(1)
+        nc.sync.dma_start(code_rows[:, 0:HALF], y_code[:, 0:HALF].bitcast(I32))
+        product(3)
+        quantize_y(2)
+        quantize_y(3)
+        nc.scalar.dma_start(code_rows[:, HALF:J], y_code[:, HALF:J].bitcast(I32))
+        for q in range(4):
+            queue = nc.sync if q % 2 == 0 else nc.scalar
+            queue.dma_start(out_2[0, 4 * q : 4 * q + 4, :].bitcast(I32), y_scale[32 * q : 32 * q + 4, :].bitcast(I32))

@@ -42,39 +42,48 @@ def tile_moe_expert_with_taps_pl_kernel(tc, xf, ta, tb, td, w_words, w_scales, r
         rw_col = keep.tile([P, PACK], F32, name="rw_col")
         ws_raw = keep.tile([P, N], U8, name="ws_raw")
         zeros = keep.tile([P, PAD], F32, name="zeros")
-        nc.vector.memset(zeros[:], 0.0)
         nc.vector.memset(ws_raw[:].bitcast(I32), 0)
+        nc.vector.memset(zeros[:], 0.0)
         nc.sync.dma_start(offsets[:], offs)
         for t in range(PACK):
             nc.sync.dma_start(window[t][:], x_rows[:, t, :])
         nc.sync.dma_start(w_raw[:], w_words[0].rearrange("p n t -> p (n t)").bitcast(I32))
         nc.scalar.dma_start(ta_sb[:], ta.rearrange("(p t) o -> p (t o)", t=PACK))
         nc.scalar.dma_start(tb_sb[:], tb.rearrange("(p t) o -> p (t o)", t=PACK))
-        nc.gpsimd.dma_start(td_sb[:], td.rearrange("(p t) o -> p (t o)", t=PACK))
-        nc.gpsimd.dma_start(rw_col[:], rw.rearrange("o (n m) -> (o n) m", m=PACK))
         xg = [keep.tile([P, PAD + J], F32, name=f"xg{t}") for t in range(PACK)]
         for t in range(PACK):
             nc.scalar.activation(xg[t][:, 0:PAD], zeros[:], COPY)
+        nc.scalar.dma_start(td_sb[:], td.rearrange("(p t) o -> p (t o)", t=PACK))
         for q in range(4):
             nc.scalar.dma_start(ws_raw[32 * q : 32 * q + 4, :].bitcast(I32), w_scales[0, 4 * q : 4 * q + 4, :].bitcast(I32))
+        nc.scalar.dma_start(rw_col[:], rw.rearrange("o (n m) -> (o n) m", m=PACK))
         ident = keep.tile([P, P], F32, name="ident")
         make_identity(nc, ident[:])
 
         rw_ps = psum.tile([P, PACK, P], F32, name="rw_ps")
         for m in range(PACK):
             nc.tensor.transpose(rw_ps[:, m, :], rw_col[:, m : m + 1].to_broadcast([P, P]), ident[:])
-        rw_all = keep.tile([P, J], F32, name="rw_all")
-        nc.scalar.copy(rw_all[:].rearrange("p (n m) -> p n m", m=PACK), rw_ps[:].rearrange("p m n -> p n m"))
 
         w_scale = keep.tile([P, N], U8, name="w_scale", align_bytes=64)
         nc.vector.tensor_copy(
             w_scale[:].rearrange("p (t m) -> p m t", t=PACK), ws_raw[:].rearrange("p (m t) -> p m t", t=PACK)
         )
 
-        own = [keep.tile([P, J], F32, name=f"own{t}") for t in range(PACK)]
+        own = [keep.tile([P, J], F32, name=f"own{t}", tag=f"own{t}") for t in range(PACK)]
         near = [keep.tile([P, PACK, HALF], F32, name=f"near{h}") for h in range(2)]
         far = [keep.tile([P, PACK, HALF], F32, name=f"far{h}") for h in range(2)]
         w_code = keep.tile([P, N], I32, name="w_code", align_bytes=64)
+
+        def tap_far(t, h):
+            j0, j1 = h * HALF, (h + 1) * HALF
+            nc.scalar.activation(far[h][:, t, :], xg[t][:, PAD - 2 + j0 : PAD - 2 + j1], COPY, scale=td_sb[:, t : t + 1])
+
+        def tap_near(t, h):
+            j0, j1 = h * HALF, (h + 1) * HALF
+            nc.scalar.activation(own[t][:, j0:j1], xg[t][:, PAD + j0 : PAD + j1], COPY, scale=ta_sb[:, t : t + 1])
+            nc.vector.scalar_tensor_tensor(
+                near[h][:, t, :], xg[t][:, PAD - 1 + j0 : PAD - 1 + j1], tb_sb[:, t : t + 1], own[t][:, j0:j1], MULT, ADD
+            )
 
         for t in range(PACK):
             for h in range(2):
@@ -82,15 +91,18 @@ def tile_moe_expert_with_taps_pl_kernel(tc, xf, ta, tb, td, w_words, w_scales, r
                 nc.vector.tensor_copy(
                     xg[t][:, PAD + j0 : PAD + j1], window[t][:].indirect(offsets[:, j0 // LIST_ROWS : j1 // LIST_ROWS])
                 )
-            for h in range(2):
-                j0, j1 = h * HALF, (h + 1) * HALF
-                nc.scalar.activation(own[t][:, j0:j1], xg[t][:, PAD + j0 : PAD + j1], COPY, scale=ta_sb[:, t : t + 1])
-                nc.vector.scalar_tensor_tensor(
-                    near[h][:, t, :], xg[t][:, PAD - 1 + j0 : PAD - 1 + j1], tb_sb[:, t : t + 1], own[t][:, j0:j1], MULT, ADD
-                )
-            for h in range(2):
-                j0, j1 = h * HALF, (h + 1) * HALF
-                nc.scalar.activation(far[h][:, t, :], xg[t][:, PAD - 2 + j0 : PAD - 2 + j1], COPY, scale=td_sb[:, t : t + 1])
+            if t < PACK - 1:
+                tap_near(t, 0)
+                tap_near(t, 1)
+                tap_far(t, 0)
+                tap_far(t, 1)
+            else:
+                for h in range(2):
+                    tap_near(t, h)
+                    tap_far(t, h)
+
+        rw_all = keep.tile([P, J], F32, name="rw_all", tag="own1")
+        nc.scalar.copy(rw_all[:].rearrange("p (n m) -> p n m", m=PACK), rw_ps[:].rearrange("p m n -> p n m"))
 
         nc.vector.tensor_copy(
             w_code[:].rearrange("p (t m) -> p m t", t=PACK), w_raw[:].rearrange("p (m t) -> p m t", t=PACK)
@@ -104,9 +116,9 @@ def tile_moe_expert_with_taps_pl_kernel(tc, xf, ta, tb, td, w_words, w_scales, r
             h, c0 = divmod(c * CHUNK, HALF)
             u_words = keep.tile([P, CHUNK, PACK], BF16, name=f"u_words{c}", align_bytes=64)
             nc.vector.tensor_tensor(
-                u_words[:].rearrange("p (c i) t -> p c t i", i=4),
-                near[h][:, :, c0 : c0 + CHUNK].rearrange("p t (c i) -> p c t i", i=4),
-                far[h][:, :, c0 : c0 + CHUNK].rearrange("p t (c i) -> p c t i", i=4),
+                u_words[:].rearrange("p (c i) t -> p c t i", i=2),
+                near[h][:, :, c0 : c0 + CHUNK].rearrange("p t (c i) -> p c t i", i=2),
+                far[h][:, :, c0 : c0 + CHUNK].rearrange("p t (c i) -> p c t i", i=2),
                 ADD,
             )
             nc.vector.quantize_mx(

@@ -42,32 +42,33 @@ def tile_moe_expert_with_taps_pl_kernel(tc, xf, ta, tb, td, w_words, w_scales, r
         rw_col = keep.tile([P, PACK], F32, name="rw_col")
         ws_raw = keep.tile([P, N], U8, name="ws_raw")
         zeros = keep.tile([P, PAD], F32, name="zeros")
-        nc.vector.memset(ws_raw[:].bitcast(I32), 0)
+        nc.gpsimd.memset(ws_raw[:].bitcast(I32), 0)
         nc.vector.memset(zeros[:], 0.0)
         nc.sync.dma_start(offsets[:], offs)
+        nc.sync.dma_start(ta_sb[:], ta.rearrange("(p t) o -> p (t o)", t=PACK))
         for t in range(PACK):
             nc.sync.dma_start(window[t][:], x_rows[:, t, :])
         nc.sync.dma_start(w_raw[:], w_words[0].rearrange("p n t -> p (n t)").bitcast(I32))
-        nc.scalar.dma_start(ta_sb[:], ta.rearrange("(p t) o -> p (t o)", t=PACK))
         nc.scalar.dma_start(tb_sb[:], tb.rearrange("(p t) o -> p (t o)", t=PACK))
+        nc.scalar.dma_start(ws_raw[0:16, :].bitcast(I32), w_scales[0].bitcast(I32))
+        nc.scalar.dma_start(td_sb[:], td.rearrange("(p t) o -> p (t o)", t=PACK))
+        nc.scalar.dma_start(rw_col[:], rw.rearrange("o (n m) -> (o n) m", m=PACK))
         xg = [keep.tile([P, PAD + J], F32, name=f"xg{t}") for t in range(PACK)]
         for t in range(PACK):
             nc.scalar.activation(xg[t][:, 0:PAD], zeros[:], COPY)
-        nc.scalar.dma_start(td_sb[:], td.rearrange("(p t) o -> p (t o)", t=PACK))
-        for q in range(4):
-            nc.scalar.dma_start(ws_raw[32 * q : 32 * q + 4, :].bitcast(I32), w_scales[0, 4 * q : 4 * q + 4, :].bitcast(I32))
-        nc.scalar.dma_start(rw_col[:], rw.rearrange("o (n m) -> (o n) m", m=PACK))
         ident = keep.tile([P, P], F32, name="ident")
         make_identity(nc, ident[:])
-
-        rw_ps = psum.tile([P, PACK, P], F32, name="rw_ps")
-        for m in range(PACK):
-            nc.tensor.transpose(rw_ps[:, m, :], rw_col[:, m : m + 1].to_broadcast([P, P]), ident[:])
 
         w_scale = keep.tile([P, N], U8, name="w_scale", align_bytes=64)
         nc.vector.tensor_copy(
             w_scale[:].rearrange("p (t m) -> p m t", t=PACK), ws_raw[:].rearrange("p (m t) -> p m t", t=PACK)
         )
+        for q in range(1, 4):
+            nc.scalar.dma_start(w_scale[32 * q : 32 * q + 4, :].bitcast(I32), w_scale[4 * q : 4 * q + 4, :].bitcast(I32))
+
+        rw_ps = psum.tile([P, PACK, P], F32, name="rw_ps")
+        for m in range(PACK):
+            nc.tensor.transpose(rw_ps[:, m, :], rw_col[:, m : m + 1].to_broadcast([P, P]), ident[:])
 
         own = [keep.tile([P, J], F32, name=f"own{t}", tag=f"own{t}") for t in range(PACK)]
         near = [keep.tile([P, PACK, HALF], F32, name=f"near{h}") for h in range(2)]
@@ -100,6 +101,7 @@ def tile_moe_expert_with_taps_pl_kernel(tc, xf, ta, tb, td, w_words, w_scales, r
                 for h in range(2):
                     tap_near(t, h)
                     tap_far(t, h)
+
 
         rw_all = keep.tile([P, J], F32, name="rw_all", tag="own1")
         nc.scalar.copy(rw_all[:].rearrange("p (n m) -> p n m", m=PACK), rw_ps[:].rearrange("p m n -> p n m"))
@@ -171,11 +173,11 @@ def tile_moe_expert_with_taps_pl_kernel(tc, xf, ta, tb, td, w_words, w_scales, r
         product(2)
         quantize_y(0)
         quantize_y(1)
-        nc.sync.dma_start(code_rows[:, 0:HALF], y_code[:, 0:HALF].bitcast(I32))
         product(3)
         quantize_y(2)
+        nc.sync.dma_start(code_rows[:, 0 : J - CHUNK], y_code[:, 0 : J - CHUNK].bitcast(I32))
         quantize_y(3)
-        nc.scalar.dma_start(code_rows[:, HALF:J], y_code[:, HALF:J].bitcast(I32))
+        nc.scalar.dma_start(code_rows[:, J - CHUNK : J], y_code[:, J - CHUNK : J].bitcast(I32))
         for q in range(4):
             queue = nc.sync if q % 2 == 0 else nc.scalar
             queue.dma_start(out_2[0, 4 * q : 4 * q + 4, :].bitcast(I32), y_scale[32 * q : 32 * q + 4, :].bitcast(I32))

from contextlib import ExitStack

import concourse.mybir as mybir
from concourse.masks import make_identity

K, T, J, N = 512, 2048, 512, 512
FLOPS = 2 * K * J * N

F32 = mybir.dt.float32
BF16 = mybir.dt.bfloat16
I32 = mybir.dt.int32
U32 = mybir.dt.uint32
U16 = mybir.dt.uint16
U8 = mybir.dt.uint8
FP8X4 = mybir.dt.float8_e4m3fn_x4
MULT = mybir.AluOpType.mult
ADD = mybir.AluOpType.add
MAX = mybir.AluOpType.max
COPY = mybir.ActivationFunctionType.Copy

P = 128
PACK = 4
PAD = 4
HALF = J // 2
CHUNK = 128
LIST_ROWS = 16


def tile_moe_expert_with_taps_pl_kernel(tc, xf, ta, tb, td, w_words, w_scales, rw, offs, out_0, out_1, out_2):
    nc = tc.nc
    with ExitStack() as ctx:
        keep = ctx.enter_context(tc.tile_pool(name="keep", bufs=1))
        psum = ctx.enter_context(tc.psum_pool(name="psum", bufs=1))

        offsets = keep.tile([P, J // LIST_ROWS], U16, name="offsets")
        x_rows = xf.rearrange("(p t) c -> p t c", t=PACK)
        window = [keep.tile([P, T], F32, name=f"window{t}") for t in range(PACK)]
        w_raw = keep.tile([P, N], I32, name="w_raw")
        ta_sb = keep.tile([P, PACK], F32, name="ta_sb")
        tb_sb = keep.tile([P, PACK], F32, name="tb_sb")
        td_sb = keep.tile([P, PACK], F32, name="td_sb")
        rw_col = keep.tile([P, PACK], F32, name="rw_col")
        ws_raw = keep.tile([P, N], U8, name="ws_raw")
        zeros = keep.tile([P, PAD], F32, name="zeros")
        nc.gpsimd.memset(ws_raw[:].bitcast(I32), 0)
        nc.vector.memset(zeros[:], 0.0)
        nc.sync.dma_start(offsets[:], offs)
        nc.sync.dma_start(ta_sb[:], ta.rearrange("(p t) o -> p (t o)", t=PACK))
        for t in range(PACK):
            nc.sync.dma_start(window[t][:], x_rows[:, t, :])
        nc.sync.dma_start(w_raw[:], w_words[0].rearrange("p n t -> p (n t)").bitcast(I32))
        nc.scalar.dma_start(tb_sb[:], tb.rearrange("(p t) o -> p (t o)", t=PACK))
        nc.scalar.dma_start(ws_raw[0:16, :].bitcast(I32), w_scales[0].bitcast(I32))
        nc.scalar.dma_start(td_sb[:], td.rearrange("(p t) o -> p (t o)", t=PACK))
        nc.scalar.dma_start(rw_col[:], rw.rearrange("o (n m) -> (o n) m", m=PACK))
        xg = [keep.tile([P, PAD + J], F32, name=f"xg{t}") for t in range(PACK)]
        for t in range(PACK):
            nc.scalar.activation(xg[t][:, 0:PAD], zeros[:], COPY)
        ident = keep.tile([P, P], F32, name="ident")
        make_identity(nc, ident[:])

        w_scale = keep.tile([P, N], U8, name="w_scale", align_bytes=64)
        nc.vector.tensor_copy(
            w_scale[:].rearrange("p (t m) -> p m t", t=PACK), ws_raw[:].rearrange("p (m t) -> p m t", t=PACK)
        )
        for q in range(1, 4):
            nc.scalar.dma_start(w_scale[32 * q : 32 * q + 4, :].bitcast(I32), w_scale[4 * q : 4 * q + 4, :].bitcast(I32))

        rw_ps = psum.tile([P, PACK, P], F32, name="rw_ps")
        for m in range(PACK):
            nc.tensor.transpose(rw_ps[:, m, :], rw_col[:, m : m + 1].to_broadcast([P, P]), ident[:])

        own = [keep.tile([P, J], F32, name=f"own{t}", tag=f"own{t}") for t in range(PACK)]
        near = [keep.tile([P, PACK, HALF], F32, name=f"near{h}") for h in range(2)]
        far = [keep.tile([P, PACK, HALF], F32, name=f"far{h}") for h in range(2)]
        w_code = keep.tile([P, N], I32, name="w_code", align_bytes=64)

        def tap_far(t, h):
            j0, j1 = h * HALF, (h + 1) * HALF
            nc.scalar.activation(far[h][:, t, :], xg[t][:, PAD - 2 + j0 : PAD - 2 + j1], COPY, scale=td_sb[:, t : t + 1])

        def tap_near(t, h):
            j0, j1 = h * HALF, (h + 1) * HALF
            nc.scalar.activation(own[t][:, j0:j1], xg[t][:, PAD + j0 : PAD + j1], COPY, scale=ta_sb[:, t : t + 1])
            nc.vector.scalar_tensor_tensor(
                near[h][:, t, :], xg[t][:, PAD - 1 + j0 : PAD - 1 + j1], tb_sb[:, t : t + 1], own[t][:, j0:j1], MULT, ADD
            )

        for t in range(PACK):
            for h in range(2):
                j0, j1 = h * HALF, (h + 1) * HALF
                nc.vector.tensor_copy(
                    xg[t][:, PAD + j0 : PAD + j1], window[t][:].indirect(offsets[:, j0 // LIST_ROWS : j1 // LIST_ROWS])
                )
            if t < PACK - 1:
                tap_near(t, 0)
                tap_near(t, 1)
                tap_far(t, 0)
                tap_far(t, 1)
            else:
                for h in range(2):
                    tap_near(t, h)
                    tap_far(t, h)


        rw_all = keep.tile([P, J], F32, name="rw_all", tag="own1")
        nc.scalar.copy(rw_all[:].rearrange("p (n m) -> p n m", m=PACK), rw_ps[:].rearrange("p m n -> p n m"))

        nc.vector.tensor_copy(
            w_code[:].rearrange("p (t m) -> p m t", t=PACK), w_raw[:].rearrange("p (m t) -> p m t", t=PACK)
        )

        chunks = J // CHUNK
        u_code = [keep.tile([P, CHUNK], U32, name=f"u_code{c}", align_bytes=64) for c in range(chunks)]
        u_scale = [keep.tile([P, CHUNK], U8, name=f"u_scale{c}", align_bytes=64) for c in range(chunks)]

        def quantize_u(c):
            h, c0 = divmod(c * CHUNK, HALF)
            u_words = keep.tile([P, CHUNK, PACK], BF16, name=f"u_words{c}", align_bytes=64)
            nc.vector.tensor_tensor(
                u_words[:].rearrange("p (c i) t -> p c t i", i=2),
                near[h][:, :, c0 : c0 + CHUNK].rearrange("p t (c i) -> p c t i", i=2),
                far[h][:, :, c0 : c0 + CHUNK].rearrange("p t (c i) -> p c t i", i=2),
                ADD,
            )
            nc.vector.quantize_mx(
                out=u_code[c][:].bitcast(FP8X4), scales=u_scale[c][:], in_=u_words[:].rearrange("p j t -> p (j t)")
            )

        y_rows = out_0.rearrange("(p t) j -> p t j", t=PACK)
        y_code = keep.tile([P, J], U32, name="y_code", align_bytes=64)
        y_scale = keep.tile([P, J], U8, name="y_scale", align_bytes=64)
        code_rows = out_1[0].rearrange("p j t -> p (j t)").bitcast(I32)
        y_words = []

        def product(c):
            acc = psum.tile([P, PACK, CHUNK], F32, name=f"acc{c}")
            for t in range(PACK):
                nc.tensor.matmul_mx(
                    out=acc[:, t, :],
                    lhsT=w_code[:, t * P : (t + 1) * P].bitcast(FP8X4),
                    lhsT_scale=w_scale[:, t * P : (t + 1) * P],
                    rhs=u_code[c][:].bitcast(FP8X4),
                    rhs_scale=u_scale[c][:],
                    start=True,
                    stop=True,
                )
            cols = slice(c * CHUNK, (c + 1) * CHUNK)
            y = keep.tile([P, PACK, CHUNK], F32, name=f"y{c}")
            nc.vector.scalar_tensor_tensor(
                y[:], acc[:], 0.0, rw_all[:, cols].unsqueeze(1).to_broadcast([P, PACK, CHUNK]), MAX, MULT
            )
            nc.sync.dma_start(y_rows[:, :, cols], y[:])
            words = keep.tile([P, CHUNK, PACK], BF16, name=f"y_words{c}", align_bytes=64)
            dst = words[:].rearrange("p (c i) t -> p c t i", i=4)
            src = y[:].rearrange("p t (c i) -> p c t i", i=4)
            if c < chunks - 1:
                nc.scalar.copy(dst, src)
            else:
                nc.vector.tensor_copy(dst, src)
            y_words.append(words)

        def quantize_y(c):
            cols = slice(c * CHUNK, (c + 1) * CHUNK)
            nc.vector.quantize_mx(
                out=y_code[:, cols].bitcast(FP8X4), scales=y_scale[:, cols], in_=y_words[c][:].rearrange("p j t -> p (j t)")
            )

        for c in range(chunks):
            quantize_u(c)
        product(0)
        product(1)
        product(2)
        quantize_y(0)
        quantize_y(1)
        product(3)
        quantize_y(2)
        nc.sync.dma_start(code_rows[:, 0 : J - CHUNK], y_code[:, 0 : J - CHUNK].bitcast(I32))
        quantize_y(3)
        nc.scalar.dma_start(code_rows[:, J - CHUNK : J], y_code[:, J - CHUNK : J].bitcast(I32))
        for q in range(4):
            queue = nc.sync if q % 2 == 0 else nc.scalar
            queue.dma_start(out_2[0, 4 * q : 4 * q + 4, :].bitcast(I32), y_scale[32 * q : 32 * q + 4, :].bitcast(I32))
